import numpy as np
import ml_dtypes


def mxq(x, axis, fmt="e4m3"):
    dtype, down = {"e4m3": (ml_dtypes.float8_e4m3fn, 7), "e5m2": (ml_dtypes.float8_e5m2, 14)}[fmt]
    v = np.moveaxis(np.asarray(x, np.float32).astype(ml_dtypes.bfloat16).astype(np.float64), axis, -1)
    blocks = v.reshape(v.shape[:-1] + (-1, 32))
    amax = np.abs(blocks).max(-1, keepdims=True)
    byte = np.maximum(np.where(amax > 0, np.frexp(amax)[1] - 1 + 127, 0) - down, 1)
    scale = np.exp2(byte - 127.0)
    codes = (blocks / scale).astype(np.float32).astype(dtype).astype(np.float64)
    return np.moveaxis((codes * scale).reshape(v.shape), -1, axis)


WIDE = False


def mx_kscale(k):
    if not WIDE:
        return np.ones(k)
    levels = np.array([10, -10, 5, -5, 0])
    if k % 512:
        return np.exp2(np.random.permutation(np.resize(levels, k // 32))).repeat(32)
    a = np.empty((k // 512, 16))
    for p in range(k // 512):
        a[p, :8] = np.random.permutation(np.resize(levels, 8))
        for g in range(8):
            far = levels[np.abs(levels - a[p, g]) >= 10]
            a[p, g + 8] = far[np.random.randint(len(far))]
    return np.exp2(a.ravel()).repeat(32)


def f64(x):
    return np.asarray(x).astype(np.float64)


def striped(idx):
    return np.tile(idx.reshape(-1, 16).T, (8, 1)).astype(np.uint16)


def unstriped(offs):
    return offs[:16].T.reshape(-1).astype(np.int64)


def striped8(idx):
    return np.concatenate([x.reshape(-1, 16).T for x in idx]).astype(np.uint16)


def runs(offs, k):
    lists = np.stack([offs[16 * r : 16 * r + 16].T.reshape(-1) for r in range(8)]).astype(np.int64)
    return lists[np.arange(k) % 512 // 64]


def pack_weight(w):
    k, n = w.shape
    w = f64(np.asarray(w, np.float32).astype(ml_dtypes.bfloat16)).reshape(k // 32, 32, n)
    amax = np.abs(w).max(1)
    byte = np.clip(np.where(amax > 0, np.frexp(amax)[1] - 1 + 127 - 7, 1), 1, 254)
    scaled = (w * np.exp2(127.0 - byte)[:, None, :]).reshape(k, n).astype(np.float32)
    words = np.ascontiguousarray(scaled.reshape(k // 512, 128, 4, n).transpose(0, 1, 3, 2)).astype(ml_dtypes.float8_e4m3fn).view(np.uint8)
    return words, np.ascontiguousarray(byte.astype(np.uint8).reshape(k // 512, 16, n))


def unpack_weight(words, scales):
    g, p, n, _ = words.shape
    vals = np.ascontiguousarray(words).view(ml_dtypes.float8_e4m3fn).astype(np.float64) * np.repeat(np.exp2(scales.astype(np.float64) - 127.0), 8, axis=1)[..., None]
    return vals.transpose(0, 1, 3, 2).reshape(g * 512, n)

def planes(y):
    n, m = y.shape
    v = y.astype(np.float32).astype(ml_dtypes.bfloat16).astype(np.float64).reshape(n // 32, 32, m)
    top = np.abs(v).max(1)
    byte = np.clip(np.where(top > 0, np.frexp(top)[1] - 1 + 127 - 7, 1), 1, 254)
    codes = (v * np.exp2(127.0 - byte)[:, None, :]).reshape(n, m).astype(np.float32).astype(ml_dtypes.float8_e4m3fn).view(np.uint8)
    words = codes.reshape(n // 512, 128, 4, m).transpose(0, 1, 3, 2)
    return np.ascontiguousarray(words), np.ascontiguousarray(byte.astype(np.uint8).reshape(n // 512, 16, m))


K, T, S, G, H, U = 512, 1024, 256, 2048, 512, 512


def setup_inputs():
    n = np.random.standard_normal
    s = mx_kscale(K)[:, None]
    packed_xT = pack_weight(n((K, T)) * s)
    packed_dT = pack_weight(n((K, G)) / s)
    perm = np.random.permutation(U)
    return {
        "x_words": packed_xT[0],
        "x_scales": packed_xT[1],
        "d_words": packed_dT[0],
        "d_scales": packed_dT[1],
        "gs": (np.random.uniform(0.5, 1.5, (K, 1)) * s).astype(np.float32),
        "offs": striped(np.random.permutation(T)[:S]),
        "k1": striped8(np.random.randint(0, G, (8, H))),
        "n1": striped(np.random.permutation(S)),
        "n2": striped(np.random.permutation(S)),
        "k2": striped8(np.random.randint(0, G, (8, H))),
        "k3": striped8(np.random.randint(0, G, (8, H))),
        "two": striped(np.random.permutation(T)[:S]),
        "n3": striped(perm[:S]),
        "n4": striped(perm[S:]),
        "n5": striped(np.random.permutation(S)),
    }


def reference(x_words, x_scales, d_words, d_scales, gs, offs, k1, n1, n2, k2, k3, two, n3, n4, n5):
    d_k2 = unpack_weight(d_words, d_scales)[np.arange(K)[:, None], runs(k2, K)]
    d_k1 = unpack_weight(d_words, d_scales)[np.arange(K)[:, None], runs(k1, K)]
    xq = unpack_weight(x_words, x_scales)[:, unstriped(offs)]
    h = 0.0625 * (d_k1.T @ xq)
    ds = np.zeros((H, S))
    ds[:, unstriped(n1)] = h
    st = np.maximum(h, ds)
    ds2 = np.zeros((H, S))
    ds2[:, unstriped(n2)] = st
    z = f64(gs) * (st - ds2)
    d_k3 = unpack_weight(d_words, d_scales)[np.arange(K)[:, None], runs(k3, K)]
    x_two = unpack_weight(x_words, x_scales)[:, unstriped(two)]
    h2 = 0.0625 * ((d_k2.T @ mxq(z, 0, "e4m3") + d_k3.T @ x_two))
    nw = h2 - h2[:, unstriped(n5)]
    ph = np.zeros((H, U))
    ph[:, unstriped(n3)] = h2
    out = ph.copy()
    out[:, unstriped(n4)] = nw
    return (out,) + planes(out)

@@ -1,0 +1,208 @@
+from contextlib import ExitStack
+
+import concourse.mybir as mybir
+
+F32 = mybir.dt.float32
+BF16 = mybir.dt.bfloat16
+U32 = mybir.dt.uint32
+I32 = mybir.dt.int32
+U16 = mybir.dt.uint16
+U8 = mybir.dt.uint8
+FP8X4 = mybir.dt.float8_e4m3fn_x4
+ALU = mybir.AluOpType
+COPY = mybir.ActivationFunctionType.Copy
+
+P = 128
+PACK = 4
+K, T, S, G, H, U = 512, 1024, 256, 2048, 512, 512
+FLOPS = 3 * 2 * K * H * S
+SIXTEENTH = 0.0625
+
+
+def deal(nc, dst, src, run):
+    nc.vector.tensor_copy(
+        out=dst.rearrange("p (t a m) -> p a t m", t=PACK, m=run),
+        in_=src.rearrange("p (a m t) -> p a t m", t=PACK, m=run),
+    )
+
+
+def lift_rows(queue, plane):
+    for i in range(1, 4):
+        queue.dma_start(out=plane[i:P:32, :].bitcast(I32), in_=plane[8 * i : P : 32, :].bitcast(I32))
+
+
+def load_scale_table(queue, table, scales):
+    rows = scales[0].bitcast(I32)
+    queue.dma_start(out=table[:].bitcast(I32), in_=rows.unsqueeze(1).to_broadcast([16, 8, rows.shape[1]]))
+
+
+def tile_picked_ctzmtsndtwinpagq_none_po_kernel(
+    tc, x_words, x_scales, d_words, d_scales, gs, offs, k1, n1, n2, k2, k3, two, n3, n4, n5, out_0, out_1, out_2
+):
+    nc = tc.nc
+    with ExitStack() as ctx:
+        lists = ctx.enter_context(tc.tile_pool(name="lists", bufs=1))
+        sb = ctx.enter_context(tc.tile_pool(name="sb", bufs=1))
+        psum = ctx.enter_context(tc.psum_pool(name="psum", bufs=1))
+
+        def tile(shape, dtype, name, tag=None):
+            return sb.tile(shape, dtype, name=name, tag=tag or name, align_bytes=64)
+
+        def load_list(src, name):
+            held = lists.tile(list(src.shape), U16, name=name)
+            nc.sync.dma_start(held[:], src)
+            return held
+
+        d_tab = tile([P, G], U32, "d_tab")
+        x_tab = tile([P, T], U32, "x_tab")
+        d_sc = tile([P, G], U8, "d_sc")
+        x_sc = tile([P, T], U8, "x_sc")
+
+        k1_l = load_list(k1, "k1_l")
+        load_scale_table(nc.scalar, d_sc, d_scales)
+        offs_l = load_list(offs, "offs_l")
+        nc.scalar.dma_start(out=d_tab[:].bitcast(I32), in_=d_words[0].rearrange("p n t -> p (n t)").bitcast(I32))
+        load_scale_table(nc.sync, x_sc, x_scales)
+        nc.scalar.dma_start(out=x_tab[:].bitcast(I32), in_=x_words[0].rearrange("p n t -> p (n t)").bitcast(I32))
+        n1_l = load_list(n1, "n1_l")
+        k3_l = load_list(k3, "k3_l")
+        k2_l = load_list(k2, "k2_l")
+        two_l = load_list(two, "two_l")
+        n2_l = load_list(n2, "n2_l")
+        n5_l = load_list(n5, "n5_l")
+        n3_l = load_list(n3, "n3_l")
+        n4_l = load_list(n4, "n4_l")
+
+        b1_raw = tile([P, H], U8, "b1_raw", "slot_g")
+        nc.vector.tensor_copy(out=b1_raw[:], in_=d_sc[:].indirect(k1_l[:]))
+        xb1_raw = tile([P, S], U8, "xb1_raw")
+        nc.vector.tensor_copy(out=xb1_raw[:], in_=x_sc[:].indirect(offs_l[:]))
+        b1 = tile([P, H + S], U8, "b1", "slot_c")
+        deal(nc, b1[:, :H], b1_raw[:], 16)
+        nc.vector.tensor_copy(out=b1[:, H:].bitcast(I32), in_=xb1_raw[:].bitcast(I32))
+        lift_rows(nc.scalar, b1)
+        gain = tile([P, PACK], F32, "gain", "slot_g")
+        nc.sync.dma_start(out=gain[:], in_=gs.rearrange("(p t) o -> p (t o)", t=PACK))
+        w1_raw = tile([P, H], U32, "w1_raw")
+        nc.vector.tensor_copy(out=w1_raw[:], in_=d_tab[:].indirect(k1_l[:]))
+        w1 = tile([P, H], U32, "w1", "slot_a")
+        deal(nc, w1[:], w1_raw[:], 4)
+        xw1 = tile([P, S], U32, "xw1", "slot_b")
+        nc.vector.tensor_copy(out=xw1[:], in_=x_tab[:].indirect(offs_l[:]))
+
+        h, ds, st, ds2 = [], [], [], []
+        for t in range(PACK):
+            cols = slice(t * P, (t + 1) * P)
+            acc = psum.tile([P, S], F32, name=f"acc1_{t}", tag=f"bank{t}")
+            nc.tensor.matmul_mx(out=acc[:], lhsT=w1[:, cols].bitcast(FP8X4), lhsT_scale=b1[:, cols],
+                                rhs=xw1[:].bitcast(FP8X4), rhs_scale=b1[:, H:], start=True, stop=True)
+            h.append(tile([P, S], F32, f"h{t}", f"slot_h{t}"))
+            nc.vector.tensor_scalar_mul(h[t][:], acc[:], SIXTEENTH)
+        for t in range(PACK):
+            ds.append(tile([P, 2 * S], F32, f"ds{t}"))
+            nc.scalar.activation(out=ds[t][:].indirect(n1_l[:]), in_=h[t][:], func=COPY)
+
+        def take_max(t):
+            st.append(tile([P, S], F32, f"st{t}"))
+            nc.vector.tensor_max(st[t][:], h[t][:], ds[t][:, :S])
+            ds2.append(tile([P, 2 * S], F32, f"ds2_{t}"))
+            nc.scalar.activation(out=ds2[t][:].indirect(n2_l[:]), in_=st[t][:], func=COPY)
+
+        zb = tile([P, S, PACK], BF16, "zb")
+
+        def make_z(t):
+            diff = tile([P, S], F32, f"diff{t}")
+            nc.vector.tensor_sub(diff[:], st[t][:], ds2[t][:, :S])
+            nc.vector.tensor_scalar_mul(zb[:, :, t], diff[:], gain[:, t : t + 1])
+
+        b23_raw = tile([P, 2 * H], U8, "b23_raw", "slot_a")
+        nc.vector.tensor_copy(out=b23_raw[:, :H], in_=d_sc[:].indirect(k3_l[:]))
+        nc.vector.tensor_copy(out=b23_raw[:, H:], in_=d_sc[:].indirect(k2_l[:]))
+        xb2_raw = tile([P, S], U8, "xb2_raw", "slot_c")
+        nc.vector.tensor_copy(out=xb2_raw[:], in_=x_sc[:].indirect(two_l[:]))
+        b23 = tile([P, 2 * H + S], U8, "b23")
+        deal(nc, b23[:, :H], b23_raw[:, :H], 16)
+        deal(nc, b23[:, H : 2 * H], b23_raw[:, H:], 16)
+        nc.vector.tensor_copy(out=b23[:, 2 * H :].bitcast(I32), in_=xb2_raw[:].bitcast(I32))
+        lift_rows(nc.sync, b23)
+        take_max(0)
+        take_max(1)
+        xw2 = tile([P, S], U32, "xw2", "slot_b")
+        nc.vector.tensor_copy(out=xw2[:], in_=x_tab[:].indirect(two_l[:]))
+        w3_raw = tile([P, H], U32, "w3_raw", "slot_h0")
+        nc.vector.tensor_copy(out=w3_raw[:], in_=d_tab[:].indirect(k3_l[:]))
+        take_max(2)
+        w3 = tile([P, H], U32, "w3")
+        deal(nc, w3[:], w3_raw[:], 4)
+        take_max(3)
+        w2_raw = tile([P, H], U32, "w2_raw", "slot_h1")
+        nc.vector.tensor_copy(out=w2_raw[:], in_=d_tab[:].indirect(k2_l[:]))
+        make_z(0)
+        w2 = tile([P, H], U32, "w2")
+        deal(nc, w2[:], w2_raw[:], 4)
+
+        halves = (slice(0, S // 2), slice(S // 2, S))
+        pieces = [(0, halves[0]), (0, halves[1])] + [(t, slice(0, S)) for t in range(1, PACK)]
+        acc2 = []
+        for j, (t, tok) in enumerate(pieces):
+            cols = slice(t * P, (t + 1) * P)
+            acc2.append(psum.tile([P, tok.stop - tok.start], F32, name=f"acc2_{j}", tag=f"bank{(PACK + j) % 8}"))
+            nc.tensor.matmul_mx(out=acc2[j][:], lhsT=w3[:, cols].bitcast(FP8X4), lhsT_scale=b23[:, cols],
+                                rhs=xw2[:, tok].bitcast(FP8X4),
+                                rhs_scale=b23[:, 2 * H + tok.start : 2 * H + tok.stop], start=True, stop=False)
+        for t in range(1, PACK - 1):
+            make_z(t)
+        last = PACK - 1
+        diff = tile([P, S], F32, "diff_last")
+        for tok in halves:
+            nc.vector.tensor_sub(diff[:, tok], st[last][:, tok], ds2[last][:, tok])
+        for tok in halves:
+            nc.vector.tensor_scalar_mul(zb[:, tok, last], diff[:, tok], gain[:, last : last + 1])
+        zw = tile([P, S], U32, "zw")
+        zs = tile([P, S], U8, "zs")
+        for tok in halves:
+            nc.vector.quantize_mx(out=zw[:, tok].bitcast(FP8X4), scales=zs[:, tok],
+                                  in_=zb[:, tok, :].rearrange("p c t -> p (c t)"))
+
+        h2 = [tile([P, 2 * S], F32, f"h2_{t}") for t in range(PACK)]
+        for j, (t, tok) in enumerate(pieces):
+            cols = slice(t * P, (t + 1) * P)
+            scale_cols = slice(H + t * P, H + (t + 1) * P)
+            nc.tensor.matmul_mx(out=acc2[j][:], lhsT=w2[:, cols].bitcast(FP8X4), lhsT_scale=b23[:, scale_cols],
+                                rhs=zw[:, tok].bitcast(FP8X4), rhs_scale=zs[:, tok], start=False, stop=True)
+            nc.vector.tensor_scalar_mul(h2[t][:, tok], acc2[j][:], SIXTEENTH)
+
+        yb = tile([P, U, PACK], BF16, "yb")
+        out_rows = out_0.rearrange("(p t) c -> t p c", t=PACK)
+        half = U // 2
+        for t in range(PACK):
+            page = tile([P, U], F32, f"page{t}")
+            early = S // 2 if t == 0 else 0
+            if early:
+                nc.scalar.activation(out=page[:].indirect(n3_l[:, : early // 16]), in_=h2[t][:, :early], func=COPY)
+            fetched = tile([P, S], F32, f"fetched{t}")
+            nc.scalar.activation(out=fetched[:], in_=h2[t][:].indirect(n5_l[:]), func=COPY)
+            nw = tile([P, S], F32, f"nw{t}")
+            nc.vector.tensor_sub(nw[:], h2[t][:, :S], fetched[:])
+            nc.scalar.activation(out=page[:].indirect(n3_l[:, early // 16 :]), in_=h2[t][:, early:S], func=COPY)
+            nc.scalar.activation(out=page[:].indirect(n4_l[:]), in_=nw[:], func=COPY)
+            nc.sync.dma_start(out=out_rows[t], in_=page[:])
+            if t < last:
+                nc.vector.tensor_copy(out=yb[:, :, t], in_=page[:])
+            else:
+                for a in range(2):
+                    cols = slice(a * half, (a + 1) * half)
+                    nc.vector.tensor_copy(out=yb[:, cols, t], in_=page[:, cols])
+
+        yw = tile([P, U], U32, "yw")
+        ys = tile([P, U], U8, "ys")
+        words_out = out_1[0].rearrange("p n t -> p (n t)").bitcast(I32)
+        for a in range(2):
+            cols = slice(a * half, (a + 1) * half)
+            nc.vector.quantize_mx(out=yw[:, cols].bitcast(FP8X4), scales=ys[:, cols],
+                                  in_=yb[:, cols, :].rearrange("p c t -> p (c t)"))
+            nc.sync.dma_start(out=words_out[:, cols], in_=yw[:, cols].bitcast(I32))
+        scales_out = out_2[0].bitcast(I32)
+        for q in range(4):
+            queue = nc.scalar if q % 2 else nc.sync
+            queue.dma_start(out=scales_out[4 * q : 4 * q + 4, :], in_=ys[32 * q : 32 * q + 4, :].bitcast(I32))

@@ -19,11 +19,16 @@ FLOPS = 3 * 2 * K * H * S
 SIXTEENTH = 0.0625
 
 
-def deal(nc, dst, src, run):
+def deal(nc, dst, src, run, slots=slice(0, PACK)):
     nc.vector.tensor_copy(
-        out=dst.rearrange("p (t a m) -> p a t m", t=PACK, m=run),
-        in_=src.rearrange("p (a m t) -> p a t m", t=PACK, m=run),
+        out=dst.rearrange("p (t a m) -> p a t m", t=PACK, m=run)[:, :, slots, :],
+        in_=src.rearrange("p (a m t) -> p a t m", t=PACK, m=run)[:, :, slots, :],
     )
+
+
+def place_rows(queue, plane, picked):
+    for i in range(4):
+        queue.dma_start(out=plane[i:P:32, :].bitcast(I32), in_=picked[8 * i : P : 32, :].bitcast(I32))
 
 
 def lift_rows(queue, plane):
@@ -61,10 +66,10 @@ def tile_picked_ctzmtsndtwinpagq_none_po_kernel(
         k1_l = load_list(k1, "k1_l")
         load_scale_table(nc.scalar, d_sc, d_scales)
         offs_l = load_list(offs, "offs_l")
+        load_scale_table(nc.scalar, x_sc, x_scales)
         nc.scalar.dma_start(out=d_tab[:].bitcast(I32), in_=d_words[0].rearrange("p n t -> p (n t)").bitcast(I32))
-        load_scale_table(nc.sync, x_sc, x_scales)
-        nc.scalar.dma_start(out=x_tab[:].bitcast(I32), in_=x_words[0].rearrange("p n t -> p (n t)").bitcast(I32))
         n1_l = load_list(n1, "n1_l")
+        nc.scalar.dma_start(out=x_tab[:].bitcast(I32), in_=x_words[0].rearrange("p n t -> p (n t)").bitcast(I32))
         k3_l = load_list(k3, "k3_l")
         k2_l = load_list(k2, "k2_l")
         two_l = load_list(two, "two_l")
@@ -72,32 +77,37 @@ def tile_picked_ctzmtsndtwinpagq_none_po_kernel(
         n5_l = load_list(n5, "n5_l")
         n3_l = load_list(n3, "n3_l")
         n4_l = load_list(n4, "n4_l")
-
-        b1_raw = tile([P, H], U8, "b1_raw", "slot_g")
-        nc.vector.tensor_copy(out=b1_raw[:], in_=d_sc[:].indirect(k1_l[:]))
-        xb1_raw = tile([P, S], U8, "xb1_raw")
-        nc.vector.tensor_copy(out=xb1_raw[:], in_=x_sc[:].indirect(offs_l[:]))
-        b1 = tile([P, H + S], U8, "b1", "slot_c")
-        deal(nc, b1[:, :H], b1_raw[:], 16)
-        nc.vector.tensor_copy(out=b1[:, H:].bitcast(I32), in_=xb1_raw[:].bitcast(I32))
-        lift_rows(nc.scalar, b1)
-        gain = tile([P, PACK], F32, "gain", "slot_g")
+        gain = tile([P, PACK], F32, "gain")
         nc.sync.dma_start(out=gain[:], in_=gs.rearrange("(p t) o -> p (t o)", t=PACK))
+
+        b1_rows = tile([P, H + S], U8, "b1_rows")
+        nc.vector.memset(b1_rows[:].bitcast(I32), 0)
+
+        b1_raw = tile([P, H + S], U8, "b1_raw")
+        nc.vector.tensor_copy(out=b1_raw[:, :H], in_=d_sc[:].indirect(k1_l[:]))
+        nc.vector.tensor_copy(out=b1_raw[:, H:], in_=x_sc[:].indirect(offs_l[:]))
+        place_rows(nc.scalar, b1_rows, b1_raw)
         w1_raw = tile([P, H], U32, "w1_raw")
         nc.vector.tensor_copy(out=w1_raw[:], in_=d_tab[:].indirect(k1_l[:]))
-        w1 = tile([P, H], U32, "w1", "slot_a")
-        deal(nc, w1[:], w1_raw[:], 4)
         xw1 = tile([P, S], U32, "xw1", "slot_b")
         nc.vector.tensor_copy(out=xw1[:], in_=x_tab[:].indirect(offs_l[:]))
+        w1 = tile([P, H], U32, "w1", "slot_a")
+        b1 = tile([P, H], U8, "b1")
+        for slots in (slice(0, 1), slice(1, PACK)):
+            deal(nc, w1[:], w1_raw[:], 4, slots)
+            deal(nc, b1[:], b1_rows[:, :H], 16, slots)
 
         h, ds, st, ds2 = [], [], [], []
         for t in range(PACK):
             cols = slice(t * P, (t + 1) * P)
             acc = psum.tile([P, S], F32, name=f"acc1_{t}", tag=f"bank{t}")
             nc.tensor.matmul_mx(out=acc[:], lhsT=w1[:, cols].bitcast(FP8X4), lhsT_scale=b1[:, cols],
-                                rhs=xw1[:].bitcast(FP8X4), rhs_scale=b1[:, H:], start=True, stop=True)
+                                rhs=xw1[:].bitcast(FP8X4), rhs_scale=b1_rows[:, H:], start=True, stop=True)
             h.append(tile([P, S], F32, f"h{t}", f"slot_h{t}"))
-            nc.vector.tensor_scalar_mul(h[t][:], acc[:], SIXTEENTH)
+            if t == 0:
+                nc.scalar.activation(out=h[t][:], in_=acc[:], func=COPY, scale=SIXTEENTH)
+            else:
+                nc.vector.tensor_scalar_mul(h[t][:], acc[:], SIXTEENTH)
         for t in range(PACK):
             ds.append(tile([P, 2 * S], F32, f"ds{t}"))
             nc.scalar.activation(out=ds[t][:].indirect(n1_l[:]), in_=h[t][:], func=COPY)
@@ -115,15 +125,14 @@ def tile_picked_ctzmtsndtwinpagq_none_po_kernel(
             nc.vector.tensor_sub(diff[:], st[t][:], ds2[t][:, :S])
             nc.vector.tensor_scalar_mul(zb[:, :, t], diff[:], gain[:, t : t + 1])
 
-        b23_raw = tile([P, 2 * H], U8, "b23_raw", "slot_a")
+        b23_raw = tile([P, 2 * H + S], U8, "b23_raw", "slot_a")
         nc.vector.tensor_copy(out=b23_raw[:, :H], in_=d_sc[:].indirect(k3_l[:]))
-        nc.vector.tensor_copy(out=b23_raw[:, H:], in_=d_sc[:].indirect(k2_l[:]))
-        xb2_raw = tile([P, S], U8, "xb2_raw", "slot_c")
-        nc.vector.tensor_copy(out=xb2_raw[:], in_=x_sc[:].indirect(two_l[:]))
+        nc.vector.tensor_copy(out=b23_raw[:, H : 2 * H], in_=d_sc[:].indirect(k2_l[:]))
+        nc.vector.tensor_copy(out=b23_raw[:, 2 * H :], in_=x_sc[:].indirect(two_l[:]))
         b23 = tile([P, 2 * H + S], U8, "b23")
         deal(nc, b23[:, :H], b23_raw[:, :H], 16)
-        deal(nc, b23[:, H : 2 * H], b23_raw[:, H:], 16)
-        nc.vector.tensor_copy(out=b23[:, 2 * H :].bitcast(I32), in_=xb2_raw[:].bitcast(I32))
+        deal(nc, b23[:, H : 2 * H], b23_raw[:, H : 2 * H], 16)
+        nc.vector.tensor_copy(out=b23[:, 2 * H :].bitcast(I32), in_=b23_raw[:, 2 * H :].bitcast(I32))
         lift_rows(nc.sync, b23)
         take_max(0)
         take_max(1)
@@ -153,7 +162,7 @@ def tile_picked_ctzmtsndtwinpagq_none_po_kernel(
         for t in range(1, PACK - 1):
             make_z(t)
         last = PACK - 1
-        diff = tile([P, S], F32, "diff_last")
+        diff = tile([P, S], F32, "diff_last", "diff2")
         for tok in halves:
             nc.vector.tensor_sub(diff[:, tok], st[last][:, tok], ds2[last][:, tok])
         for tok in halves:
@@ -170,7 +179,10 @@ def tile_picked_ctzmtsndtwinpagq_none_po_kernel(
             scale_cols = slice(H + t * P, H + (t + 1) * P)
             nc.tensor.matmul_mx(out=acc2[j][:], lhsT=w2[:, cols].bitcast(FP8X4), lhsT_scale=b23[:, scale_cols],
                                 rhs=zw[:, tok].bitcast(FP8X4), rhs_scale=zs[:, tok], start=False, stop=True)
-            nc.vector.tensor_scalar_mul(h2[t][:, tok], acc2[j][:], SIXTEENTH)
+            if j == 0:
+                nc.scalar.activation(out=h2[t][:, tok], in_=acc2[j][:], func=COPY, scale=SIXTEENTH)
+            else:
+                nc.vector.tensor_scalar_mul(h2[t][:, tok], acc2[j][:], SIXTEENTH)
 
         yb = tile([P, U, PACK], BF16, "yb")
         out_rows = out_0.rearrange("(p t) c -> t p c", t=PACK)

from contextlib import ExitStack

import concourse.mybir as mybir

F32 = mybir.dt.float32
BF16 = mybir.dt.bfloat16
U32 = mybir.dt.uint32
I32 = mybir.dt.int32
U16 = mybir.dt.uint16
U8 = mybir.dt.uint8
FP8X4 = mybir.dt.float8_e4m3fn_x4
ALU = mybir.AluOpType
COPY = mybir.ActivationFunctionType.Copy

P = 128
PACK = 4
K, T, S, G, H, U = 512, 1024, 256, 2048, 512, 512
FLOPS = 3 * 2 * K * H * S
SIXTEENTH = 0.0625


def deal(nc, dst, src, run, slots=slice(0, PACK)):
    nc.vector.tensor_copy(
        out=dst.rearrange("p (t a m) -> p a t m", t=PACK, m=run)[:, :, slots, :],
        in_=src.rearrange("p (a m t) -> p a t m", t=PACK, m=run)[:, :, slots, :],
    )


def place_rows(queue, plane, picked):
    for i in range(4):
        queue.dma_start(out=plane[i:P:32, :].bitcast(I32), in_=picked[8 * i : P : 32, :].bitcast(I32))


def lift_rows(queue, plane):
    for i in range(1, 4):
        queue.dma_start(out=plane[i:P:32, :].bitcast(I32), in_=plane[8 * i : P : 32, :].bitcast(I32))


def load_scale_table(queue, table, scales):
    rows = scales[0].bitcast(I32)
    queue.dma_start(out=table[:].bitcast(I32), in_=rows.unsqueeze(1).to_broadcast([16, 8, rows.shape[1]]))


def tile_picked_ctzmtsndtwinpagq_none_po_kernel(
    tc, x_words, x_scales, d_words, d_scales, gs, offs, k1, n1, n2, k2, k3, two, n3, n4, n5, out_0, out_1, out_2
):
    nc = tc.nc
    with ExitStack() as ctx:
        lists = ctx.enter_context(tc.tile_pool(name="lists", bufs=1))
        sb = ctx.enter_context(tc.tile_pool(name="sb", bufs=1))
        psum = ctx.enter_context(tc.psum_pool(name="psum", bufs=1))

        def tile(shape, dtype, name, tag=None):
            return sb.tile(shape, dtype, name=name, tag=tag or name, align_bytes=64)

        def load_list(src, name):
            held = lists.tile(list(src.shape), U16, name=name)
            nc.sync.dma_start(held[:], src)
            return held

        d_tab = tile([P, G], U32, "d_tab")
        x_tab = tile([P, T], U32, "x_tab")
        d_sc = tile([P, G], U8, "d_sc")
        x_sc = tile([P, T], U8, "x_sc")

        k1_l = load_list(k1, "k1_l")
        load_scale_table(nc.scalar, d_sc, d_scales)
        offs_l = load_list(offs, "offs_l")
        load_scale_table(nc.scalar, x_sc, x_scales)
        nc.scalar.dma_start(out=d_tab[:].bitcast(I32), in_=d_words[0].rearrange("p n t -> p (n t)").bitcast(I32))
        n1_l = load_list(n1, "n1_l")
        nc.scalar.dma_start(out=x_tab[:].bitcast(I32), in_=x_words[0].rearrange("p n t -> p (n t)").bitcast(I32))
        k3_l = load_list(k3, "k3_l")
        k2_l = load_list(k2, "k2_l")
        two_l = load_list(two, "two_l")
        n2_l = load_list(n2, "n2_l")
        n5_l = load_list(n5, "n5_l")
        n3_l = load_list(n3, "n3_l")
        n4_l = load_list(n4, "n4_l")
        gain = tile([P, PACK], F32, "gain")
        nc.sync.dma_start(out=gain[:], in_=gs.rearrange("(p t) o -> p (t o)", t=PACK))

        b1_rows = tile([P, H + S], U8, "b1_rows")
        nc.vector.memset(b1_rows[:].bitcast(I32), 0)

        b1_raw = tile([P, H + S], U8, "b1_raw")
        nc.vector.tensor_copy(out=b1_raw[:, :H], in_=d_sc[:].indirect(k1_l[:]))
        nc.vector.tensor_copy(out=b1_raw[:, H:], in_=x_sc[:].indirect(offs_l[:]))
        place_rows(nc.scalar, b1_rows, b1_raw)
        w1_raw = tile([P, H], U32, "w1_raw")
        nc.vector.tensor_copy(out=w1_raw[:], in_=d_tab[:].indirect(k1_l[:]))
        xw1 = tile([P, S], U32, "xw1", "slot_b")
        nc.vector.tensor_copy(out=xw1[:], in_=x_tab[:].indirect(offs_l[:]))
        w1 = tile([P, H], U32, "w1", "slot_a")
        b1 = tile([P, H], U8, "b1")
        for slots in (slice(0, 1), slice(1, PACK)):
            deal(nc, w1[:], w1_raw[:], 4, slots)
            deal(nc, b1[:], b1_rows[:, :H], 16, slots)

        h, ds, st, ds2 = [], [], [], []
        for t in range(PACK):
            cols = slice(t * P, (t + 1) * P)
            acc = psum.tile([P, S], F32, name=f"acc1_{t}", tag=f"bank{t}")
            nc.tensor.matmul_mx(out=acc[:], lhsT=w1[:, cols].bitcast(FP8X4), lhsT_scale=b1[:, cols],
                                rhs=xw1[:].bitcast(FP8X4), rhs_scale=b1_rows[:, H:], start=True, stop=True)
            h.append(tile([P, S], F32, f"h{t}", f"slot_h{t}"))
            if t == 0:
                nc.scalar.activation(out=h[t][:], in_=acc[:], func=COPY, scale=SIXTEENTH)
            else:
                nc.vector.tensor_scalar_mul(h[t][:], acc[:], SIXTEENTH)
        for t in range(PACK):
            ds.append(tile([P, 2 * S], F32, f"ds{t}"))
            nc.scalar.activation(out=ds[t][:].indirect(n1_l[:]), in_=h[t][:], func=COPY)

        def take_max(t):
            st.append(tile([P, S], F32, f"st{t}"))
            nc.vector.tensor_max(st[t][:], h[t][:], ds[t][:, :S])
            ds2.append(tile([P, 2 * S], F32, f"ds2_{t}"))
            nc.scalar.activation(out=ds2[t][:].indirect(n2_l[:]), in_=st[t][:], func=COPY)

        zb = tile([P, S, PACK], BF16, "zb")

        def make_z(t):
            diff = tile([P, S], F32, f"diff{t}")
            nc.vector.tensor_sub(diff[:], st[t][:], ds2[t][:, :S])
            nc.vector.tensor_scalar_mul(zb[:, :, t], diff[:], gain[:, t : t + 1])

        b23_raw = tile([P, 2 * H + S], U8, "b23_raw", "slot_a")
        nc.vector.tensor_copy(out=b23_raw[:, :H], in_=d_sc[:].indirect(k3_l[:]))
        nc.vector.tensor_copy(out=b23_raw[:, H : 2 * H], in_=d_sc[:].indirect(k2_l[:]))
        nc.vector.tensor_copy(out=b23_raw[:, 2 * H :], in_=x_sc[:].indirect(two_l[:]))
        b23 = tile([P, 2 * H + S], U8, "b23")
        deal(nc, b23[:, :H], b23_raw[:, :H], 16)
        deal(nc, b23[:, H : 2 * H], b23_raw[:, H : 2 * H], 16)
        nc.vector.tensor_copy(out=b23[:, 2 * H :].bitcast(I32), in_=b23_raw[:, 2 * H :].bitcast(I32))
        lift_rows(nc.sync, b23)
        take_max(0)
        take_max(1)
        xw2 = tile([P, S], U32, "xw2", "slot_b")
        nc.vector.tensor_copy(out=xw2[:], in_=x_tab[:].indirect(two_l[:]))
        w3_raw = tile([P, H], U32, "w3_raw", "slot_h0")
        nc.vector.tensor_copy(out=w3_raw[:], in_=d_tab[:].indirect(k3_l[:]))
        take_max(2)
        w3 = tile([P, H], U32, "w3")
        deal(nc, w3[:], w3_raw[:], 4)
        take_max(3)
        w2_raw = tile([P, H], U32, "w2_raw", "slot_h1")
        nc.vector.tensor_copy(out=w2_raw[:], in_=d_tab[:].indirect(k2_l[:]))
        make_z(0)
        w2 = tile([P, H], U32, "w2")
        deal(nc, w2[:], w2_raw[:], 4)

        halves = (slice(0, S // 2), slice(S // 2, S))
        pieces = [(0, halves[0]), (0, halves[1])] + [(t, slice(0, S)) for t in range(1, PACK)]
        acc2 = []
        for j, (t, tok) in enumerate(pieces):
            cols = slice(t * P, (t + 1) * P)
            acc2.append(psum.tile([P, tok.stop - tok.start], F32, name=f"acc2_{j}", tag=f"bank{(PACK + j) % 8}"))
            nc.tensor.matmul_mx(out=acc2[j][:], lhsT=w3[:, cols].bitcast(FP8X4), lhsT_scale=b23[:, cols],
                                rhs=xw2[:, tok].bitcast(FP8X4),
                                rhs_scale=b23[:, 2 * H + tok.start : 2 * H + tok.stop], start=True, stop=False)
        for t in range(1, PACK - 1):
            make_z(t)
        last = PACK - 1
        diff = tile([P, S], F32, "diff_last", "diff2")
        for tok in halves:
            nc.vector.tensor_sub(diff[:, tok], st[last][:, tok], ds2[last][:, tok])
        for tok in halves:
            nc.vector.tensor_scalar_mul(zb[:, tok, last], diff[:, tok], gain[:, last : last + 1])
        zw = tile([P, S], U32, "zw")
        zs = tile([P, S], U8, "zs")
        for tok in halves:
            nc.vector.quantize_mx(out=zw[:, tok].bitcast(FP8X4), scales=zs[:, tok],
                                  in_=zb[:, tok, :].rearrange("p c t -> p (c t)"))

        h2 = [tile([P, 2 * S], F32, f"h2_{t}") for t in range(PACK)]
        for j, (t, tok) in enumerate(pieces):
            cols = slice(t * P, (t + 1) * P)
            scale_cols = slice(H + t * P, H + (t + 1) * P)
            nc.tensor.matmul_mx(out=acc2[j][:], lhsT=w2[:, cols].bitcast(FP8X4), lhsT_scale=b23[:, scale_cols],
                                rhs=zw[:, tok].bitcast(FP8X4), rhs_scale=zs[:, tok], start=False, stop=True)
            if j == 0:
                nc.scalar.activation(out=h2[t][:, tok], in_=acc2[j][:], func=COPY, scale=SIXTEENTH)
            else:
                nc.vector.tensor_scalar_mul(h2[t][:, tok], acc2[j][:], SIXTEENTH)

        yb = tile([P, U, PACK], BF16, "yb")
        out_rows = out_0.rearrange("(p t) c -> t p c", t=PACK)
        half = U // 2
        for t in range(PACK):
            page = tile([P, U], F32, f"page{t}")
            early = S // 2 if t == 0 else 0
            if early:
                nc.scalar.activation(out=page[:].indirect(n3_l[:, : early // 16]), in_=h2[t][:, :early], func=COPY)
            fetched = tile([P, S], F32, f"fetched{t}")
            nc.scalar.activation(out=fetched[:], in_=h2[t][:].indirect(n5_l[:]), func=COPY)
            nw = tile([P, S], F32, f"nw{t}")
            nc.vector.tensor_sub(nw[:], h2[t][:, :S], fetched[:])
            nc.scalar.activation(out=page[:].indirect(n3_l[:, early // 16 :]), in_=h2[t][:, early:S], func=COPY)
            nc.scalar.activation(out=page[:].indirect(n4_l[:]), in_=nw[:], func=COPY)
            nc.sync.dma_start(out=out_rows[t], in_=page[:])
            if t < last:
                nc.vector.tensor_copy(out=yb[:, :, t], in_=page[:])
            else:
                for a in range(2):
                    cols = slice(a * half, (a + 1) * half)
                    nc.vector.tensor_copy(out=yb[:, cols, t], in_=page[:, cols])

        yw = tile([P, U], U32, "yw")
        ys = tile([P, U], U8, "ys")
        words_out = out_1[0].rearrange("p n t -> p (n t)").bitcast(I32)
        for a in range(2):
            cols = slice(a * half, (a + 1) * half)
            nc.vector.quantize_mx(out=yw[:, cols].bitcast(FP8X4), scales=ys[:, cols],
                                  in_=yb[:, cols, :].rearrange("p c t -> p (c t)"))
            nc.sync.dma_start(out=words_out[:, cols], in_=yw[:, cols].bitcast(I32))
        scales_out = out_2[0].bitcast(I32)
        for q in range(4):
            queue = nc.scalar if q % 2 else nc.sync
            queue.dma_start(out=scales_out[4 * q : 4 * q + 4, :], in_=ys[32 * q : 32 * q + 4, :].bitcast(I32))
